import numpy as np
import ml_dtypes


def mxq(x, axis, fmt="e4m3"):
    dtype, down = {"e4m3": (ml_dtypes.float8_e4m3fn, 7), "e5m2": (ml_dtypes.float8_e5m2, 14)}[fmt]
    v = np.moveaxis(np.asarray(x, np.float32).astype(ml_dtypes.bfloat16).astype(np.float64), axis, -1)
    blocks = v.reshape(v.shape[:-1] + (-1, 32))
    amax = np.abs(blocks).max(-1, keepdims=True)
    byte = np.maximum(np.where(amax > 0, np.frexp(amax)[1] - 1 + 127, 0) - down, 1)
    scale = np.exp2(byte - 127.0)
    codes = (blocks / scale).astype(np.float32).astype(dtype).astype(np.float64)
    return np.moveaxis((codes * scale).reshape(v.shape), -1, axis)


WIDE = False


def mx_kscale(k):
    if not WIDE:
        return np.ones(k)
    levels = np.array([10, -10, 5, -5, 0])
    if k % 512:
        return np.exp2(np.random.permutation(np.resize(levels, k // 32))).repeat(32)
    a = np.empty((k // 512, 16))
    for p in range(k // 512):
        a[p, :8] = np.random.permutation(np.resize(levels, 8))
        for g in range(8):
            far = levels[np.abs(levels - a[p, g]) >= 10]
            a[p, g + 8] = far[np.random.randint(len(far))]
    return np.exp2(a.ravel()).repeat(32)


def f64(x):
    return np.asarray(x).astype(np.float64)


def striped8(idx):
    return np.concatenate([v.reshape(-1, 16).T for v in idx]).astype(np.uint16)


def unstriped8(offs):
    return np.stack([offs[16 * g:16 * g + 16].T.reshape(-1) for g in range(8)]).astype(np.int64)


E2M1 = np.array([0.0, 0.5, 1.0, 1.5, 2.0, 3.0, 4.0, 6.0, -0.0, -0.5, -1.0, -1.5, -2.0, -3.0, -4.0, -6.0])


def pack_weight(w, fmt):
    k, n = w.shape
    w = f64(np.asarray(w, np.float32).astype(ml_dtypes.bfloat16)).reshape(k // 32, 32, n)
    amax = np.abs(w).max(1)
    if fmt == "e4m3":
        byte = np.frexp(amax)[1] - 1 + 127 - 7
    else:
        mant, ex = np.frexp(amax / 6.0)
        byte = np.where(mant > 0.5, ex, ex - 1) + 127
    byte = np.clip(np.where(amax > 0, byte, 1), 1, 254)
    scaled = (w * np.exp2(127.0 - byte)[:, None, :]).reshape(k, n).astype(np.float32)
    by_word = np.ascontiguousarray(scaled.reshape(k // 512, 128, 4, n).transpose(0, 1, 3, 2))
    if fmt == "e4m3":
        words = by_word.astype(ml_dtypes.float8_e4m3fn).view(np.uint8)
    else:
        c = by_word.astype(ml_dtypes.float4_e2m1fn).view(np.uint8) & 0xF
        words = (c[..., 0::2] | (c[..., 1::2] << 4)).reshape(k // 512, 128, 2 * n)
    return np.ascontiguousarray(words), np.ascontiguousarray(byte.astype(np.uint8).reshape(k // 512, 16, n))


def unpack_weight(words, scales, fmt):
    g, _, n = scales.shape
    words = np.ascontiguousarray(words).reshape(g, 128, n, -1)
    if fmt == "e4m3":
        vals = words.view(ml_dtypes.float8_e4m3fn).astype(np.float64)
    else:
        nib = np.empty((g, 128, n, 4), np.uint8)
        nib[..., 0::2] = words & 0xF
        nib[..., 1::2] = words >> 4
        vals = E2M1[nib]
    vals = vals * np.repeat(np.exp2(scales.astype(np.float64) - 127.0), 8, axis=1)[..., None]
    return vals.transpose(0, 1, 3, 2).reshape(g * 512, n)


def silu(v):
    return v / (1.0 + np.exp(-np.maximum(v, -700.0)))


K, M, T, S = 2048, 128, 2048, 512


def setup_inputs():
    n = np.random.standard_normal
    s = mx_kscale(K)[:, None]
    w = n((K, M)) / np.sqrt(K) / s
    w4 = pack_weight(w, "e2m1")
    rest = w - unpack_weight(*w4, "e2m1")
    p_r8 = pack_weight(rest, "e4m3")
    return {
        "xT": (n((K, T)) * s).astype(np.float32),
        "w4_words": w4[0],
        "w4_scales": w4[1],
        "r8_words": p_r8[0],
        "r8_scales": p_r8[1],
        "wgt": np.repeat(np.random.uniform(0.5, 2.0, (8, S)), 16, axis=0).astype(np.float32),
        "b": (0.3 * n(128)).astype(np.float32),
        "offs": striped8(np.stack([np.random.permutation(T)[:S] for _ in range(8)])),
    }


def reference(xT, w4_words, w4_scales, r8_words, r8_scales, wgt, b, offs):
    idx = unstriped8(offs)
    group = np.arange(K) % 512 // 64
    xg = f64(wgt)[np.arange(K) // 4 % 128] * f64(xT)[np.arange(K)[:, None], idx[group]]
    xT_ = mxq(xg, 0, "e4m3")
    w4_ = unpack_weight(w4_words, w4_scales, "e2m1")
    r8_ = unpack_weight(r8_words, r8_scales, "e4m3")
    y = w4_.T @ xT_ + r8_.T @ xT_
    return silu(y + f64(b)[:, None])

@@ -1,0 +1,156 @@
+from contextlib import ExitStack
+
+import concourse.mybir as mybir
+
+F32 = mybir.dt.float32
+BF16 = mybir.dt.bfloat16
+I32 = mybir.dt.int32
+U32 = mybir.dt.uint32
+U16 = mybir.dt.uint16
+U8 = mybir.dt.uint8
+FP8X4 = mybir.dt.float8_e4m3fn_x4
+FP4X4 = mybir.dt.float4_e2m1fn_x4
+MULT = mybir.AluOpType.mult
+SILU = mybir.ActivationFunctionType.Silu
+
+K, M, T, S = 2048, 128, 2048, 512
+P = 128
+PACK = 4
+PASSES = K // (P * PACK)
+HALF = 256
+PIECE = 128
+PIECES = S // PIECE
+LATE = 2
+FLOPS = 2 * 2 * K * M * S
+
+
+def tile_list_heads_silu_kernel(tc, xT, w4_words, w4_scales, r8_words, r8_scales, wgt, b, offs, out):
+    nc = tc.nc
+    with ExitStack() as ctx:
+        lists = ctx.enter_context(tc.tile_pool(name="lists", bufs=1))
+        keep = ctx.enter_context(tc.tile_pool(name="keep", bufs=1))
+        work = ctx.enter_context(tc.tile_pool(name="work", bufs=4))
+        psum = ctx.enter_context(tc.psum_pool(name="psum", bufs=1))
+
+        offsets = lists.tile([P, S // 16], U16, name="offsets")
+        nc.sync.dma_start(offsets[:], offs)
+        weights = keep.tile([P, S], F32, name="weights")
+        nc.sync.dma_start(weights[:], wgt)
+
+        w4 = keep.tile([P, PASSES, 2 * M], U8, name="w4", align_bytes=64)
+        r8 = keep.tile([P, PASSES, 4 * M], U8, name="r8", align_bytes=64)
+        w4s = keep.tile([P, PASSES, M], U8, name="w4s", align_bytes=64)
+        r8s = keep.tile([P, PASSES, M], U8, name="r8s", align_bytes=64)
+        bias = keep.tile([P, 1], F32, name="bias")
+        w4_src = w4_words.rearrange("a p c -> p a c")
+        r8_src = r8_words.rearrange("a p n i -> p a (n i)")
+
+        nc.vector.memset(w4s[:].bitcast(I32), 0)
+        nc.vector.memset(r8s[:].bitcast(I32), 0)
+        nc.gpsimd.dma_start(w4[:, 0:LATE, :].bitcast(I32), w4_src[:, 0:LATE, :].bitcast(I32))
+        nc.gpsimd.dma_start(r8[:, 0:LATE, :].bitcast(I32), r8_src[:, 0:LATE, :].bitcast(I32))
+        for plane, scales in ((w4s, w4_scales), (r8s, r8_scales)):
+            for q in range(4):
+                nc.gpsimd.dma_start(
+                    plane[32 * q : 32 * q + 4, :, :].bitcast(I32),
+                    scales[:, 4 * q : 4 * q + 4, :].rearrange("a r n -> r a n").bitcast(I32),
+                )
+        nc.gpsimd.dma_start(bias[:], b.rearrange("(p o) -> p o", o=1))
+
+        warm = keep.tile([P, 1], F32, name="warm")
+        nc.vector.memset(warm[:], 0.0)
+        warmed = keep.tile([P, 1], F32, name="warmed")
+        nc.scalar.activation(warmed[:], warm[:], SILU)
+
+        planes = []
+        for a in range(PASSES):
+            rows = xT[a * P * PACK : (a + 1) * P * PACK, :].rearrange("(p i) t -> p i t", i=PACK)
+            for i in range(PACK):
+                plane = keep.tile([P, T], F32, name=f"plane{a}_{i}")
+                nc.sync.dma_start(plane[:], rows[:, i, :])
+                planes.append(plane)
+        nc.sync.dma_start(w4[:, LATE:, :].bitcast(I32), w4_src[:, LATE:, :].bitcast(I32))
+        nc.sync.dma_start(r8[:, LATE:, :].bitcast(I32), r8_src[:, LATE:, :].bitcast(I32))
+
+        sums = [psum.tile([P, PIECE], F32, name=f"sum{q}") for q in range(PIECES)]
+
+        def pick(dst, a, i, j0, n):
+            nc.vector.tensor_tensor(
+                dst,
+                planes[PACK * a + i][:].indirect(offsets[:, j0 // 16 : (j0 + n) // 16]),
+                weights[:, j0 : j0 + n],
+                MULT,
+            )
+
+        def multiply(q, a, codes, scales):
+            nc.tensor.matmul_mx(
+                out=sums[q][:],
+                lhsT=w4[:, a, :].bitcast(FP4X4),
+                lhsT_scale=w4s[:, a, :],
+                rhs=codes.bitcast(FP8X4),
+                rhs_scale=scales,
+                start=(a == 0),
+                stop=False,
+            )
+            nc.tensor.matmul_mx(
+                out=sums[q][:],
+                lhsT=r8[:, a, :].bitcast(FP8X4),
+                lhsT_scale=r8s[:, a, :],
+                rhs=codes.bitcast(FP8X4),
+                rhs_scale=scales,
+                start=False,
+                stop=(a == PASSES - 1),
+            )
+
+        def finish_pass(a, grouped):
+            for h in range(2):
+                codes = work.tile([P, HALF], U32, name="codes", align_bytes=64)
+                scales = work.tile([P, HALF], U8, name="scales", align_bytes=64)
+                nc.vector.quantize_mx(
+                    out=codes[:].bitcast(FP8X4), scales=scales[:], in_=grouped[h][:].rearrange("p n i -> p (n i)")
+                )
+                for q in range(2):
+                    cols = slice(q * PIECE, (q + 1) * PIECE)
+                    multiply(2 * h + q, a, codes[:, cols], scales[:, cols])
+
+        pending = None
+        for a in range(PASSES - 1):
+            picked = [work.tile([P, PACK, HALF], F32, name="picked") for h in range(2)]
+            for i in range(PACK):
+                for h in range(2):
+                    pick(picked[h][:, i, :], a, i, h * HALF, HALF)
+                if i == 1 and pending is not None:
+                    finish_pass(a - 1, pending)
+            pending = []
+            for h in range(2):
+                grouped = work.tile([P, HALF, PACK], BF16, name="grouped", align_bytes=64)
+                nc.scalar.copy(grouped[:], picked[h][:].rearrange("p i n -> p n i"))
+                pending.append(grouped)
+
+        a = PASSES - 1
+        last = [keep.tile([P, PIECE, PACK], BF16, name=f"last{q}", align_bytes=64) for q in range(PIECES)]
+        pair = [keep.tile([P, 2, HALF], F32, name=f"pair{h}") for h in range(2)]
+        for i in range(2):
+            for h in range(2):
+                pick(pair[h][:, i, :], a, i, h * HALF, HALF)
+        finish_pass(a - 1, pending)
+        for q in range(PIECES):
+            cols = slice(q % 2 * PIECE, (q % 2 + 1) * PIECE)
+            nc.scalar.copy(last[q][:, :, 0:2], pair[q // 2][:, :, cols].rearrange("p i n -> p n i"))
+        for i in (2, 3):
+            single = [keep.tile([P, PIECE], F32, name=f"single{i}_{q}") for q in range(PIECES)]
+            for q in range(PIECES):
+                pick(single[q][:], a, i, q * PIECE, PIECE)
+                if q < 2:
+                    nc.scalar.copy(last[q][:, :, i], single[q][:])
+            for q in (2, 3):
+                nc.vector.tensor_copy(last[q][:, :, i], single[q][:])
+
+        for q in range(PIECES):
+            codes = keep.tile([P, PIECE], U32, name=f"last_codes{q}", align_bytes=64)
+            scales = keep.tile([P, PIECE], U8, name=f"last_scales{q}", align_bytes=64)
+            nc.vector.quantize_mx(out=codes[:].bitcast(FP8X4), scales=scales[:], in_=last[q][:].rearrange("p n i -> p (n i)"))
+            multiply(q, a, codes[:], scales[:])
+            result = keep.tile([P, PIECE], F32, name=f"result{q}")
+            nc.scalar.activation(result[:], sums[q][:], SILU, bias=bias[:])
+            nc.sync.dma_start(out[:, q * PIECE : (q + 1) * PIECE], result[:])

@@ -34,8 +34,11 @@ def tile_list_heads_silu_kernel(tc, xT, w4_words, w4_scales, r8_words, r8_scales
 
         offsets = lists.tile([P, S // 16], U16, name="offsets")
         nc.sync.dma_start(offsets[:], offs)
-        weights = keep.tile([P, S], F32, name="weights")
-        nc.sync.dma_start(weights[:], wgt)
+        rows8 = keep.tile([P, S], F32, name="rows8", align_bytes=64)
+        nc.vector.memset(rows8[:], 0.0)
+        turned = keep.tile([P, S], F32, name="turned", align_bytes=64)
+        spread = keep.tile([P, S], F32, name="spread", align_bytes=64)
+        weights = keep.tile([P, S], F32, name="weights", align_bytes=64)
 
         w4 = keep.tile([P, PASSES, 2 * M], U8, name="w4", align_bytes=64)
         r8 = keep.tile([P, PASSES, 4 * M], U8, name="r8", align_bytes=64)
@@ -47,14 +50,15 @@ def tile_list_heads_silu_kernel(tc, xT, w4_words, w4_scales, r8_words, r8_scales
 
         nc.vector.memset(w4s[:].bitcast(I32), 0)
         nc.vector.memset(r8s[:].bitcast(I32), 0)
-        nc.gpsimd.dma_start(w4[:, 0:LATE, :].bitcast(I32), w4_src[:, 0:LATE, :].bitcast(I32))
-        nc.gpsimd.dma_start(r8[:, 0:LATE, :].bitcast(I32), r8_src[:, 0:LATE, :].bitcast(I32))
+        nc.scalar.dma_start(w4[:, 0:LATE, :].bitcast(I32), w4_src[:, 0:LATE, :].bitcast(I32))
+        nc.scalar.dma_start(r8[:, 0:LATE, :].bitcast(I32), r8_src[:, 0:LATE, :].bitcast(I32))
         for plane, scales in ((w4s, w4_scales), (r8s, r8_scales)):
             for q in range(4):
                 nc.gpsimd.dma_start(
                     plane[32 * q : 32 * q + 4, :, :].bitcast(I32),
                     scales[:, 4 * q : 4 * q + 4, :].rearrange("a r n -> r a n").bitcast(I32),
                 )
+
         nc.gpsimd.dma_start(bias[:], b.rearrange("(p o) -> p o", o=1))
 
         warm = keep.tile([P, 1], F32, name="warm")
@@ -67,10 +71,21 @@ def tile_list_heads_silu_kernel(tc, xT, w4_words, w4_scales, r8_words, r8_scales
             rows = xT[a * P * PACK : (a + 1) * P * PACK, :].rearrange("(p i) t -> p i t", i=PACK)
             for i in range(PACK):
                 plane = keep.tile([P, T], F32, name=f"plane{a}_{i}")
-                nc.sync.dma_start(plane[:], rows[:, i, :])
+                queue = nc.scalar if i % 2 == 1 and a < PASSES - 1 else nc.sync
+                queue.dma_start(plane[:], rows[:, i, :])
                 planes.append(plane)
+                if a == 0 and i == 0:
+                    nc.sync.dma_start(rows8[0:P:16, :], wgt[0:P:16, :])
         nc.sync.dma_start(w4[:, LATE:, :].bitcast(I32), w4_src[:, LATE:, :].bitcast(I32))
         nc.sync.dma_start(r8[:, LATE:, :].bitcast(I32), r8_src[:, LATE:, :].bitcast(I32))
+
+
+        nc.vector.transpose(turned[:], rows8[:])
+        nc.vector.tensor_copy(
+            spread[:].rearrange("p (c s) -> p c s", s=16),
+            turned[:].rearrange("p (c s) -> p c s", s=16)[:, :, 0:1].to_broadcast([P, S // 16, 16]),
+        )
+        nc.vector.transpose(weights[:], spread[:])
 
         sums = [psum.tile([P, PIECE], F32, name=f"sum{q}") for q in range(PIECES)]
 
@@ -104,8 +119,8 @@ def tile_list_heads_silu_kernel(tc, xT, w4_words, w4_scales, r8_words, r8_scales
 
         def finish_pass(a, grouped):
             for h in range(2):
-                codes = work.tile([P, HALF], U32, name="codes", align_bytes=64)
-                scales = work.tile([P, HALF], U8, name="scales", align_bytes=64)
+                codes = keep.tile([P, HALF], U32, name=f"codes{a}_{h}", align_bytes=64)
+                scales = keep.tile([P, HALF], U8, name=f"scales{a}_{h}", align_bytes=64)
                 nc.vector.quantize_mx(
                     out=codes[:].bitcast(FP8X4), scales=scales[:], in_=grouped[h][:].rearrange("p n i -> p (n i)")
                 )
@@ -143,7 +158,7 @@ def tile_list_heads_silu_kernel(tc, xT, w4_words, w4_scales, r8_words, r8_scales
                 pick(single[q][:], a, i, q * PIECE, PIECE)
                 if q < 2:
                     nc.scalar.copy(last[q][:, :, i], single[q][:])
-            for q in (2, 3):
+            for q in range(2, PIECES):
                 nc.vector.tensor_copy(last[q][:, :, i], single[q][:])
 
         for q in range(PIECES):

from contextlib import ExitStack

import concourse.mybir as mybir

F32 = mybir.dt.float32
BF16 = mybir.dt.bfloat16
I32 = mybir.dt.int32
U32 = mybir.dt.uint32
U16 = mybir.dt.uint16
U8 = mybir.dt.uint8
FP8X4 = mybir.dt.float8_e4m3fn_x4
FP4X4 = mybir.dt.float4_e2m1fn_x4
MULT = mybir.AluOpType.mult
SILU = mybir.ActivationFunctionType.Silu

K, M, T, S = 2048, 128, 2048, 512
P = 128
PACK = 4
PASSES = K // (P * PACK)
HALF = 256
PIECE = 128
PIECES = S // PIECE
LATE = 2
FLOPS = 2 * 2 * K * M * S


def tile_list_heads_silu_kernel(tc, xT, w4_words, w4_scales, r8_words, r8_scales, wgt, b, offs, out):
    nc = tc.nc
    with ExitStack() as ctx:
        lists = ctx.enter_context(tc.tile_pool(name="lists", bufs=1))
        keep = ctx.enter_context(tc.tile_pool(name="keep", bufs=1))
        work = ctx.enter_context(tc.tile_pool(name="work", bufs=4))
        psum = ctx.enter_context(tc.psum_pool(name="psum", bufs=1))

        offsets = lists.tile([P, S // 16], U16, name="offsets")
        nc.sync.dma_start(offsets[:], offs)
        rows8 = keep.tile([P, S], F32, name="rows8", align_bytes=64)
        nc.vector.memset(rows8[:], 0.0)
        turned = keep.tile([P, S], F32, name="turned", align_bytes=64)
        spread = keep.tile([P, S], F32, name="spread", align_bytes=64)
        weights = keep.tile([P, S], F32, name="weights", align_bytes=64)

        w4 = keep.tile([P, PASSES, 2 * M], U8, name="w4", align_bytes=64)
        r8 = keep.tile([P, PASSES, 4 * M], U8, name="r8", align_bytes=64)
        w4s = keep.tile([P, PASSES, M], U8, name="w4s", align_bytes=64)
        r8s = keep.tile([P, PASSES, M], U8, name="r8s", align_bytes=64)
        bias = keep.tile([P, 1], F32, name="bias")
        w4_src = w4_words.rearrange("a p c -> p a c")
        r8_src = r8_words.rearrange("a p n i -> p a (n i)")

        nc.vector.memset(w4s[:].bitcast(I32), 0)
        nc.vector.memset(r8s[:].bitcast(I32), 0)
        nc.scalar.dma_start(w4[:, 0:LATE, :].bitcast(I32), w4_src[:, 0:LATE, :].bitcast(I32))
        nc.scalar.dma_start(r8[:, 0:LATE, :].bitcast(I32), r8_src[:, 0:LATE, :].bitcast(I32))
        for plane, scales in ((w4s, w4_scales), (r8s, r8_scales)):
            for q in range(4):
                nc.gpsimd.dma_start(
                    plane[32 * q : 32 * q + 4, :, :].bitcast(I32),
                    scales[:, 4 * q : 4 * q + 4, :].rearrange("a r n -> r a n").bitcast(I32),
                )

        nc.gpsimd.dma_start(bias[:], b.rearrange("(p o) -> p o", o=1))

        warm = keep.tile([P, 1], F32, name="warm")
        nc.vector.memset(warm[:], 0.0)
        warmed = keep.tile([P, 1], F32, name="warmed")
        nc.scalar.activation(warmed[:], warm[:], SILU)

        planes = []
        for a in range(PASSES):
            rows = xT[a * P * PACK : (a + 1) * P * PACK, :].rearrange("(p i) t -> p i t", i=PACK)
            for i in range(PACK):
                plane = keep.tile([P, T], F32, name=f"plane{a}_{i}")
                queue = nc.scalar if i % 2 == 1 and a < PASSES - 1 else nc.sync
                queue.dma_start(plane[:], rows[:, i, :])
                planes.append(plane)
                if a == 0 and i == 0:
                    nc.sync.dma_start(rows8[0:P:16, :], wgt[0:P:16, :])
        nc.sync.dma_start(w4[:, LATE:, :].bitcast(I32), w4_src[:, LATE:, :].bitcast(I32))
        nc.sync.dma_start(r8[:, LATE:, :].bitcast(I32), r8_src[:, LATE:, :].bitcast(I32))


        nc.vector.transpose(turned[:], rows8[:])
        nc.vector.tensor_copy(
            spread[:].rearrange("p (c s) -> p c s", s=16),
            turned[:].rearrange("p (c s) -> p c s", s=16)[:, :, 0:1].to_broadcast([P, S // 16, 16]),
        )
        nc.vector.transpose(weights[:], spread[:])

        sums = [psum.tile([P, PIECE], F32, name=f"sum{q}") for q in range(PIECES)]

        def pick(dst, a, i, j0, n):
            nc.vector.tensor_tensor(
                dst,
                planes[PACK * a + i][:].indirect(offsets[:, j0 // 16 : (j0 + n) // 16]),
                weights[:, j0 : j0 + n],
                MULT,
            )

        def multiply(q, a, codes, scales):
            nc.tensor.matmul_mx(
                out=sums[q][:],
                lhsT=w4[:, a, :].bitcast(FP4X4),
                lhsT_scale=w4s[:, a, :],
                rhs=codes.bitcast(FP8X4),
                rhs_scale=scales,
                start=(a == 0),
                stop=False,
            )
            nc.tensor.matmul_mx(
                out=sums[q][:],
                lhsT=r8[:, a, :].bitcast(FP8X4),
                lhsT_scale=r8s[:, a, :],
                rhs=codes.bitcast(FP8X4),
                rhs_scale=scales,
                start=False,
                stop=(a == PASSES - 1),
            )

        def finish_pass(a, grouped):
            for h in range(2):
                codes = keep.tile([P, HALF], U32, name=f"codes{a}_{h}", align_bytes=64)
                scales = keep.tile([P, HALF], U8, name=f"scales{a}_{h}", align_bytes=64)
                nc.vector.quantize_mx(
                    out=codes[:].bitcast(FP8X4), scales=scales[:], in_=grouped[h][:].rearrange("p n i -> p (n i)")
                )
                for q in range(2):
                    cols = slice(q * PIECE, (q + 1) * PIECE)
                    multiply(2 * h + q, a, codes[:, cols], scales[:, cols])

        pending = None
        for a in range(PASSES - 1):
            picked = [work.tile([P, PACK, HALF], F32, name="picked") for h in range(2)]
            for i in range(PACK):
                for h in range(2):
                    pick(picked[h][:, i, :], a, i, h * HALF, HALF)
                if i == 1 and pending is not None:
                    finish_pass(a - 1, pending)
            pending = []
            for h in range(2):
                grouped = work.tile([P, HALF, PACK], BF16, name="grouped", align_bytes=64)
                nc.scalar.copy(grouped[:], picked[h][:].rearrange("p i n -> p n i"))
                pending.append(grouped)

        a = PASSES - 1
        last = [keep.tile([P, PIECE, PACK], BF16, name=f"last{q}", align_bytes=64) for q in range(PIECES)]
        pair = [keep.tile([P, 2, HALF], F32, name=f"pair{h}") for h in range(2)]
        for i in range(2):
            for h in range(2):
                pick(pair[h][:, i, :], a, i, h * HALF, HALF)
        finish_pass(a - 1, pending)
        for q in range(PIECES):
            cols = slice(q % 2 * PIECE, (q % 2 + 1) * PIECE)
            nc.scalar.copy(last[q][:, :, 0:2], pair[q // 2][:, :, cols].rearrange("p i n -> p n i"))
        for i in (2, 3):
            single = [keep.tile([P, PIECE], F32, name=f"single{i}_{q}") for q in range(PIECES)]
            for q in range(PIECES):
                pick(single[q][:], a, i, q * PIECE, PIECE)
                if q < 2:
                    nc.scalar.copy(last[q][:, :, i], single[q][:])
            for q in range(2, PIECES):
                nc.vector.tensor_copy(last[q][:, :, i], single[q][:])

        for q in range(PIECES):
            codes = keep.tile([P, PIECE], U32, name=f"last_codes{q}", align_bytes=64)
            scales = keep.tile([P, PIECE], U8, name=f"last_scales{q}", align_bytes=64)
            nc.vector.quantize_mx(out=codes[:].bitcast(FP8X4), scales=scales[:], in_=last[q][:].rearrange("p n i -> p (n i)"))
            multiply(q, a, codes[:], scales[:])
            result = keep.tile([P, PIECE], F32, name=f"result{q}")
            nc.scalar.activation(result[:], sums[q][:], SILU, bias=bias[:])
            nc.sync.dma_start(out[:, q * PIECE : (q + 1) * PIECE], result[:])
